import numpy as np
import ml_dtypes

BF16 = ml_dtypes.bfloat16


def bf(x):
    return np.asarray(x, np.float32).astype(BF16)


def f32(x):
    return np.asarray(x, np.float32)


def f64(x):
    return np.asarray(x).astype(np.float64)


def striped(idx):
    return np.concatenate([l.reshape(-1, 16).T for l in idx])


def rows(idx, k):
    return np.tile(np.repeat(idx, 16, axis=0), (k // (16 * 8), 1))


def look(tab, idx):
    return np.take_along_axis(f64(tab), rows(idx, len(tab)), axis=1)


K, S, H, V, N, M = 128, 2048, 256, 1024, 1024, 128


def setup_inputs():
    return {"z": bf(np.random.standard_normal((H, S))), "wt": bf(np.random.standard_normal((H, K)) / np.sqrt(H)), "base": f32(1.0 * np.random.standard_normal((K, V))), "w": bf(np.random.standard_normal((K, M)) / np.sqrt(K)), "b": f32(0.5 * np.random.standard_normal((M, 1))), "offs": striped(np.stack([np.random.permutation(S)[:N] for _ in range(8)]))}


def reference(z, wt, base, w, b, offs):
    idx = np.stack([g.T.reshape(-1) for g in np.split(offs, 8)])
    tab = f64(wt).T @ f64(z)
    x = f64(base) + look(tab, idx)
    return np.maximum(f64(w).T @ x + f64(b), 0.0)

@@ -1,0 +1,67 @@
+import concourse.mybir as mybir
+
+F32 = mybir.dt.float32
+BF16 = mybir.dt.bfloat16
+U16 = mybir.dt.uint16
+ADD = mybir.AluOpType.add
+RELU = mybir.ActivationFunctionType.Relu
+
+P = 128
+H = 256
+S = 2048
+N = 1024
+BANK = 512
+PIECE = 512
+
+FLOPS = 2 * H * P * S + P * N + 2 * P * P * N
+
+
+def tile_lookup_pjadd_relu_kernel(tc, z, wt, base, w, b, offs, out):
+    nc = tc.nc
+    passes = H // P
+    with (
+        tc.tile_pool(name="held", bufs=1) as held,
+        tc.tile_pool(name="ring", bufs=2) as ring,
+        tc.psum_pool(name="psum_tab", bufs=4) as psum_tab,
+        tc.psum_pool(name="psum_out", bufs=2) as psum_out,
+    ):
+        offsets = held.tile([P, N // 16], U16, name="offsets")
+        z_sb = held.tile([P, passes, S], BF16, name="z_sb")
+        wt_sb = held.tile([P, passes, P], BF16, name="wt_sb")
+        base_sb = held.tile([P, N], F32, name="base_sb")
+        w_sb = held.tile([P, P], BF16, name="w_sb")
+        b_sb = held.tile([P, 1], F32, name="b_sb")
+        tab = held.tile([P, S], F32, name="tab")
+
+        z_rows = z.rearrange("(k p) s -> p k s", p=P)
+        nc.scalar.dma_start(wt_sb[:], wt.rearrange("(k p) r -> p k r", p=P))
+        for c in range(S // BANK):
+            columns = slice(c * BANK, (c + 1) * BANK)
+            nc.sync.dma_start(z_sb[:, :, columns], z_rows[:, :, columns])
+        nc.sync.dma_start(offsets[:], offs)
+        nc.scalar.dma_start(base_sb[:], base)
+        nc.scalar.dma_start(w_sb[:], w)
+        nc.scalar.dma_start(b_sb[:], b)
+
+        for c in range(S // BANK):
+            columns = slice(c * BANK, (c + 1) * BANK)
+            bank = psum_tab.tile([P, BANK], F32, name="bank")
+            for k in range(passes):
+                nc.tensor.matmul(bank[:], wt_sb[:, k, :], z_sb[:, k, columns], start=k == 0, stop=k == passes - 1)
+            if c % 2 == 0:
+                nc.scalar.copy(tab[:, columns], bank[:])
+            else:
+                nc.vector.tensor_copy(tab[:, columns], bank[:])
+
+        for i in range(N // PIECE):
+            piece = slice(i * PIECE, (i + 1) * PIECE)
+            entries = offsets[:, i * PIECE // 16 : (i + 1) * PIECE // 16]
+            x = ring.tile([P, PIECE], F32, name="x")
+            nc.vector.tensor_tensor(x[:], tab[:].indirect(entries), base_sb[:, piece], ADD)
+            x_bf = ring.tile([P, PIECE], BF16, name="x_bf")
+            nc.scalar.copy(x_bf[:], x[:])
+            product = psum_out.tile([P, PIECE], F32, name="product")
+            nc.tensor.matmul(product[:], w_sb[:], x_bf[:], start=True, stop=True)
+            y = ring.tile([P, PIECE], F32, name="y")
+            nc.scalar.activation(y[:], product[:], RELU, bias=b_sb[:])
+            nc.sync.dma_start(out[:, piece], y[:])

@@ -4,14 +4,16 @@ F32 = mybir.dt.float32
 BF16 = mybir.dt.bfloat16
 U16 = mybir.dt.uint16
 ADD = mybir.AluOpType.add
+MAX = mybir.AluOpType.max
 RELU = mybir.ActivationFunctionType.Relu
 
 P = 128
 H = 256
 S = 2048
 N = 1024
-BANK = 512
+CHUNK = 512
 PIECE = 512
+HALF = 256
 
 FLOPS = 2 * H * P * S + P * N + 2 * P * P * N
 
@@ -21,8 +23,8 @@ def tile_lookup_pjadd_relu_kernel(tc, z, wt, base, w, b, offs, out):
     passes = H // P
     with (
         tc.tile_pool(name="held", bufs=1) as held,
-        tc.tile_pool(name="ring", bufs=2) as ring,
-        tc.psum_pool(name="psum_tab", bufs=4) as psum_tab,
+        tc.tile_pool(name="ring", bufs=N // HALF) as ring,
+        tc.psum_pool(name="psum_tab", bufs=3) as psum_tab,
         tc.psum_pool(name="psum_out", bufs=2) as psum_out,
     ):
         offsets = held.tile([P, N // 16], U16, name="offsets")
@@ -35,33 +37,44 @@ def tile_lookup_pjadd_relu_kernel(tc, z, wt, base, w, b, offs, out):
 
         z_rows = z.rearrange("(k p) s -> p k s", p=P)
         nc.scalar.dma_start(wt_sb[:], wt.rearrange("(k p) r -> p k r", p=P))
-        for c in range(S // BANK):
-            columns = slice(c * BANK, (c + 1) * BANK)
+        for c in range(S // CHUNK):
+            columns = slice(c * CHUNK, (c + 1) * CHUNK)
             nc.sync.dma_start(z_sb[:, :, columns], z_rows[:, :, columns])
         nc.sync.dma_start(offsets[:], offs)
-        nc.scalar.dma_start(base_sb[:], base)
+        nc.sync.dma_start(base_sb[:], base)
         nc.scalar.dma_start(w_sb[:], w)
         nc.scalar.dma_start(b_sb[:], b)
 
-        for c in range(S // BANK):
-            columns = slice(c * BANK, (c + 1) * BANK)
-            bank = psum_tab.tile([P, BANK], F32, name="bank")
+        for c in range(S // CHUNK):
+            left = slice(c * CHUNK, c * CHUNK + HALF)
+            right = slice(c * CHUNK + HALF, (c + 1) * CHUNK)
+            bank_left = psum_tab.tile([P, HALF], F32, name="bank_left")
+            bank_right = psum_tab.tile([P, HALF], F32, name="bank_right")
             for k in range(passes):
-                nc.tensor.matmul(bank[:], wt_sb[:, k, :], z_sb[:, k, columns], start=k == 0, stop=k == passes - 1)
-            if c % 2 == 0:
-                nc.scalar.copy(tab[:, columns], bank[:])
-            else:
-                nc.vector.tensor_copy(tab[:, columns], bank[:])
+                first, last = k == 0, k == passes - 1
+                nc.tensor.matmul(bank_left[:], wt_sb[:, k, :], z_sb[:, k, left], start=first, stop=last)
+                nc.tensor.matmul(bank_right[:], wt_sb[:, k, :], z_sb[:, k, right], start=first, stop=last)
+            nc.scalar.copy(tab[:, left], bank_left[:])
+            nc.vector.tensor_copy(tab[:, right], bank_right[:])
 
         for i in range(N // PIECE):
-            piece = slice(i * PIECE, (i + 1) * PIECE)
+            last_piece = i == N // PIECE - 1
             entries = offsets[:, i * PIECE // 16 : (i + 1) * PIECE // 16]
             x = ring.tile([P, PIECE], F32, name="x")
-            nc.vector.tensor_tensor(x[:], tab[:].indirect(entries), base_sb[:, piece], ADD)
-            x_bf = ring.tile([P, PIECE], BF16, name="x_bf")
-            nc.scalar.copy(x_bf[:], x[:])
-            product = psum_out.tile([P, PIECE], F32, name="product")
-            nc.tensor.matmul(product[:], w_sb[:], x_bf[:], start=True, stop=True)
-            y = ring.tile([P, PIECE], F32, name="y")
-            nc.scalar.activation(y[:], product[:], RELU, bias=b_sb[:])
-            nc.sync.dma_start(out[:, piece], y[:])
+            nc.vector.tensor_tensor(x[:], tab[:].indirect(entries), base_sb[:, i * PIECE : (i + 1) * PIECE], ADD)
+
+            for h in range(PIECE // HALF):
+                half = slice(h * HALF, (h + 1) * HALF)
+                x_bf = ring.tile([P, HALF], BF16, name="x_bf")
+                if last_piece:
+                    nc.vector.tensor_copy(x_bf[:], x[:, half])
+                else:
+                    nc.scalar.copy(x_bf[:], x[:, half])
+                product = psum_out.tile([P, HALF], F32, name="product")
+                nc.tensor.matmul(product[:], w_sb[:], x_bf[:], start=True, stop=True)
+                y = ring.tile([P, HALF], F32, name="y")
+                if last_piece and h == 1:
+                    nc.vector.tensor_scalar(y[:], product[:], b_sb[:], 0.0, ADD, MAX)
+                else:
+                    nc.scalar.activation(y[:], product[:], RELU, bias=b_sb[:])
+                nc.sync.dma_start(out[:, i * PIECE + h * HALF : i * PIECE + (h + 1) * HALF], y[:])

@@ -39,12 +39,20 @@ def tile_lookup_pjadd_relu_kernel(tc, z, wt, base, w, b, offs, out):
         nc.scalar.dma_start(wt_sb[:], wt.rearrange("(k p) r -> p k r", p=P))
         for c in range(S // CHUNK):
             columns = slice(c * CHUNK, (c + 1) * CHUNK)
-            nc.sync.dma_start(z_sb[:, :, columns], z_rows[:, :, columns])
+            queue = nc.sync if c % 2 == 0 else nc.scalar
+            queue.dma_start(z_sb[:, :, columns], z_rows[:, :, columns])
         nc.sync.dma_start(offsets[:], offs)
-        nc.sync.dma_start(base_sb[:], base)
+        for i in range(N // PIECE):
+            piece = slice(i * PIECE, (i + 1) * PIECE)
+            nc.sync.dma_start(base_sb[:, piece], base[:, piece])
         nc.scalar.dma_start(w_sb[:], w)
         nc.scalar.dma_start(b_sb[:], b)
 
+        zeros = held.tile([P, HALF], BF16, name="zeros")
+        nc.vector.memset(zeros[:], 0.0)
+        warm = psum_out.tile([P, HALF], F32, name="warm", tag="product")
+        for i in range(8):
+            nc.tensor.matmul(warm[:], zeros[:, :P], zeros[:], start=True, stop=True)
         for c in range(S // CHUNK):
             left = slice(c * CHUNK, c * CHUNK + HALF)
             right = slice(c * CHUNK + HALF, (c + 1) * CHUNK)

@@ -39,8 +39,7 @@ def tile_lookup_pjadd_relu_kernel(tc, z, wt, base, w, b, offs, out):
         nc.scalar.dma_start(wt_sb[:], wt.rearrange("(k p) r -> p k r", p=P))
         for c in range(S // CHUNK):
             columns = slice(c * CHUNK, (c + 1) * CHUNK)
-            queue = nc.sync if c % 2 == 0 else nc.scalar
-            queue.dma_start(z_sb[:, :, columns], z_rows[:, :, columns])
+            nc.sync.dma_start(z_sb[:, :, columns], z_rows[:, :, columns])
         nc.sync.dma_start(offsets[:], offs)
         for i in range(N // PIECE):
             piece = slice(i * PIECE, (i + 1) * PIECE)

import concourse.mybir as mybir

F32 = mybir.dt.float32
BF16 = mybir.dt.bfloat16
U16 = mybir.dt.uint16
ADD = mybir.AluOpType.add
MAX = mybir.AluOpType.max
RELU = mybir.ActivationFunctionType.Relu

P = 128
H = 256
S = 2048
N = 1024
CHUNK = 512
PIECE = 512
HALF = 256

FLOPS = 2 * H * P * S + P * N + 2 * P * P * N


def tile_lookup_pjadd_relu_kernel(tc, z, wt, base, w, b, offs, out):
    nc = tc.nc
    passes = H // P
    with (
        tc.tile_pool(name="held", bufs=1) as held,
        tc.tile_pool(name="ring", bufs=N // HALF) as ring,
        tc.psum_pool(name="psum_tab", bufs=3) as psum_tab,
        tc.psum_pool(name="psum_out", bufs=2) as psum_out,
    ):
        offsets = held.tile([P, N // 16], U16, name="offsets")
        z_sb = held.tile([P, passes, S], BF16, name="z_sb")
        wt_sb = held.tile([P, passes, P], BF16, name="wt_sb")
        base_sb = held.tile([P, N], F32, name="base_sb")
        w_sb = held.tile([P, P], BF16, name="w_sb")
        b_sb = held.tile([P, 1], F32, name="b_sb")
        tab = held.tile([P, S], F32, name="tab")

        z_rows = z.rearrange("(k p) s -> p k s", p=P)
        nc.scalar.dma_start(wt_sb[:], wt.rearrange("(k p) r -> p k r", p=P))
        for c in range(S // CHUNK):
            columns = slice(c * CHUNK, (c + 1) * CHUNK)
            nc.sync.dma_start(z_sb[:, :, columns], z_rows[:, :, columns])
        nc.sync.dma_start(offsets[:], offs)
        for i in range(N // PIECE):
            piece = slice(i * PIECE, (i + 1) * PIECE)
            nc.sync.dma_start(base_sb[:, piece], base[:, piece])
        nc.scalar.dma_start(w_sb[:], w)
        nc.scalar.dma_start(b_sb[:], b)

        zeros = held.tile([P, HALF], BF16, name="zeros")
        nc.vector.memset(zeros[:], 0.0)
        warm = psum_out.tile([P, HALF], F32, name="warm", tag="product")
        for i in range(8):
            nc.tensor.matmul(warm[:], zeros[:, :P], zeros[:], start=True, stop=True)
        for c in range(S // CHUNK):
            left = slice(c * CHUNK, c * CHUNK + HALF)
            right = slice(c * CHUNK + HALF, (c + 1) * CHUNK)
            bank_left = psum_tab.tile([P, HALF], F32, name="bank_left")
            bank_right = psum_tab.tile([P, HALF], F32, name="bank_right")
            for k in range(passes):
                first, last = k == 0, k == passes - 1
                nc.tensor.matmul(bank_left[:], wt_sb[:, k, :], z_sb[:, k, left], start=first, stop=last)
                nc.tensor.matmul(bank_right[:], wt_sb[:, k, :], z_sb[:, k, right], start=first, stop=last)
            nc.scalar.copy(tab[:, left], bank_left[:])
            nc.vector.tensor_copy(tab[:, right], bank_right[:])

        for i in range(N // PIECE):
            last_piece = i == N // PIECE - 1
            entries = offsets[:, i * PIECE // 16 : (i + 1) * PIECE // 16]
            x = ring.tile([P, PIECE], F32, name="x")
            nc.vector.tensor_tensor(x[:], tab[:].indirect(entries), base_sb[:, i * PIECE : (i + 1) * PIECE], ADD)

            for h in range(PIECE // HALF):
                half = slice(h * HALF, (h + 1) * HALF)
                x_bf = ring.tile([P, HALF], BF16, name="x_bf")
                if last_piece:
                    nc.vector.tensor_copy(x_bf[:], x[:, half])
                else:
                    nc.scalar.copy(x_bf[:], x[:, half])
                product = psum_out.tile([P, HALF], F32, name="product")
                nc.tensor.matmul(product[:], w_sb[:], x_bf[:], start=True, stop=True)
                y = ring.tile([P, HALF], F32, name="y")
                if last_piece and h == 1:
                    nc.vector.tensor_scalar(y[:], product[:], b_sb[:], 0.0, ADD, MAX)
                else:
                    nc.scalar.activation(y[:], product[:], RELU, bias=b_sb[:])
                nc.sync.dma_start(out[:, i * PIECE + h * HALF : i * PIECE + (h + 1) * HALF], y[:])
